import numpy as np
import ml_dtypes


def mxq(x, axis, fmt="e4m3"):
    dtype, down = {"e4m3": (ml_dtypes.float8_e4m3fn, 7), "e5m2": (ml_dtypes.float8_e5m2, 14)}[fmt]
    v = np.moveaxis(np.asarray(x, np.float32).astype(ml_dtypes.bfloat16).astype(np.float64), axis, -1)
    blocks = v.reshape(v.shape[:-1] + (-1, 32))
    amax = np.abs(blocks).max(-1, keepdims=True)
    byte = np.maximum(np.where(amax > 0, np.frexp(amax)[1] - 1 + 127, 0) - down, 1)
    scale = np.exp2(byte - 127.0)
    codes = (blocks / scale).astype(np.float32).astype(dtype).astype(np.float64)
    return np.moveaxis((codes * scale).reshape(v.shape), -1, axis)


WIDE = False


def mx_kscale(k):
    if not WIDE:
        return np.ones(k)
    levels = np.array([10, -10, 5, -5, 0])
    if k % 512:
        return np.exp2(np.random.permutation(np.resize(levels, k // 32))).repeat(32)
    a = np.empty((k // 512, 16))
    for p in range(k // 512):
        a[p, :8] = np.random.permutation(np.resize(levels, 8))
        for g in range(8):
            far = levels[np.abs(levels - a[p, g]) >= 10]
            a[p, g + 8] = far[np.random.randint(len(far))]
    return np.exp2(a.ravel()).repeat(32)


def f64(x):
    return np.asarray(x).astype(np.float64)


def striped(idx):
    return np.tile(np.asarray(idx).reshape(-1, 16).T, (8, 1)).astype(np.uint16)


def unstriped(offs):
    return offs[:16].T.reshape(-1).astype(np.int64)


E2M1 = np.array([0.0, 0.5, 1.0, 1.5, 2.0, 3.0, 4.0, 6.0, -0.0, -0.5, -1.0, -1.5, -2.0, -3.0, -4.0, -6.0])


def pack_weight(w, fmt):
    k, n = w.shape
    w = f64(np.asarray(w, np.float32).astype(ml_dtypes.bfloat16)).reshape(k // 32, 32, n)
    amax = np.abs(w).max(1)
    if fmt == "e4m3":
        byte = np.frexp(amax)[1] - 1 + 127 - 7
    else:
        mant, ex = np.frexp(amax / 6.0)
        byte = np.where(mant > 0.5, ex, ex - 1) + 127
    byte = np.clip(np.where(amax > 0, byte, 1), 1, 254)
    scaled = (w * np.exp2(127.0 - byte)[:, None, :]).reshape(k, n).astype(np.float32)
    by_word = np.ascontiguousarray(scaled.reshape(k // 512, 128, 4, n).transpose(0, 1, 3, 2))
    if fmt == "e4m3":
        words = by_word.astype(ml_dtypes.float8_e4m3fn).view(np.uint8)
    else:
        c = by_word.astype(ml_dtypes.float4_e2m1fn).view(np.uint8) & 0xF
        words = (c[..., 0::2] | (c[..., 1::2] << 4)).reshape(k // 512, 128, 2 * n)
    return np.ascontiguousarray(words), np.ascontiguousarray(byte.astype(np.uint8).reshape(k // 512, 16, n))


def unpack_weight(words, scales, fmt):
    g, _, n = scales.shape
    words = np.ascontiguousarray(words).reshape(g, 128, n, -1)
    if fmt == "e4m3":
        vals = words.view(ml_dtypes.float8_e4m3fn).astype(np.float64)
    else:
        nib = np.empty((g, 128, n, 4), np.uint8)
        nib[..., 0::2] = words & 0xF
        nib[..., 1::2] = words >> 4
        vals = E2M1[nib]
    vals = vals * np.repeat(np.exp2(scales.astype(np.float64) - 127.0), 8, axis=1)[..., None]
    return vals.transpose(0, 1, 3, 2).reshape(g * 512, n)


def sigmoid(v):
    return 1.0 / (1.0 + np.exp(-v))


D, T, I, Q, E, Z, M = 512, 1024, 512, 512, 512, 1024, 1024


def setup_inputs():
    n = np.random.standard_normal
    idx = np.random.permutation(T)[:I]
    idx2 = np.random.permutation(Z)[:I]
    idx3 = np.random.permutation(M)[:I]
    fd = mx_kscale(D)
    fq = mx_kscale(Q)
    keysp = pack_weight(n((D, T)) / fd[:, None], "e2m1")
    return {
        "query": (n((D, Q)) * 1.0 / np.sqrt(D) * fd[:, None]).astype(np.float32),
        "query2": (n((D, Q)) * 1.0 / np.sqrt(D) * fd[:, None]).astype(np.float32),
        "keys_words": keysp[0],
        "keys_scales": keysp[1],
        "pages": (n((D, Z)) / fd[:, None]).astype(np.float32),
        "qs": (np.random.uniform(0.5, 2.0, (Q, 1)) * fq[:, None]).astype(np.float32),
        "msgs": (n((Q, E)) * 1 / np.sqrt(Q) / fq[:, None]).astype(np.float32),
        "old": (n((E, M)) * 1.0).astype(np.float32),
        "fade": (np.random.uniform(0.3, 0.9, (1, M))).astype(np.float32),
        "offs": striped(idx),
        "offs2": striped(idx2),
        "offs3": striped(idx3),
    }


def reference(query, query2, keys_words, keys_scales, pages, qs, msgs, old, fade, offs, offs2, offs3):
    idx = unstriped(offs)
    idx2 = unstriped(offs2)
    idx3 = unstriped(offs3)
    keysu = unpack_weight(keys_words, keys_scales, "e2m1")
    queryq = mxq(f64(query), 0, "e4m3")
    a = queryq.T @ keysu
    query2q = mxq(f64(query2), 0, "e4m3")
    pagesq = mxq(f64(pages), 0, "e4m3")
    h0 = query2q.T @ pagesq
    s = np.maximum(a[:, idx], h0[:, idx2])
    w = sigmoid(s)
    wq = w * f64(qs)
    msgsq = mxq(f64(msgs), 0, "e4m3")
    wqq = mxq(wq, 0, "e4m3")
    dl = msgsq.T @ wqq
    df = np.zeros((E, M))
    df[:, idx3] = dl
    y = f64(old) * f64(fade) + df
    return y

@@ -1,0 +1,207 @@
+from contextlib import ExitStack
+
+import concourse.mybir as mybir
+
+D, T, I, Q, E, Z, M = 512, 1024, 512, 512, 512, 1024, 1024
+FLOPS = 2 * D * Q * T + 2 * D * Q * Z + 2 * Q * E * I
+
+F32 = mybir.dt.float32
+BF16 = mybir.dt.bfloat16
+I32 = mybir.dt.int32
+U32 = mybir.dt.uint32
+U16 = mybir.dt.uint16
+U8 = mybir.dt.uint8
+FP8X4 = mybir.dt.float8_e4m3fn_x4
+FP4X4 = mybir.dt.float4_e2m1fn_x4
+ALU = mybir.AluOpType
+ACT = mybir.ActivationFunctionType
+
+P = 128
+PACK = 4
+BANK = 512
+HALF = I // 2
+LIST_COLS = HALF // 16
+
+
+def tile_attend_crosslarger_delivered_lean_kernel(
+    tc, query, query2, keys_words, keys_scales, pages, qs, msgs, old, fade, offs, offs2, offs3, out
+):
+    nc = tc.nc
+    with ExitStack() as ctx:
+        held = ctx.enter_context(tc.tile_pool(name="held", bufs=1))
+        psum = ctx.enter_context(tc.psum_pool(name="psum", bufs=8))
+
+        def by_rows(x):
+            return x.rearrange("(p t) c -> p t c", t=PACK)
+
+        def operand(name, cols):
+            grouped = held.tile([P, cols * PACK], BF16, name=name + "_bf", align_bytes=64)
+            codes = held.tile([P, cols], U32, name=name + "_codes", align_bytes=64)
+            scales = held.tile([P, cols], U8, name=name + "_scales", align_bytes=64)
+            return grouped, codes, scales
+
+        def quantise(op, c0, c1):
+            grouped, codes, scales = op
+            nc.vector.quantize_mx(
+                out=codes[:, c0:c1].bitcast(FP8X4), scales=scales[:, c0:c1], in_=grouped[:, PACK * c0 : PACK * c1]
+            )
+
+        def weave(op, raw):
+            nc.vector.tensor_copy(
+                out=op[0][:].rearrange("p (c i t) -> p c t i", i=4, t=PACK),
+                in_=raw[:].rearrange("p t (c i) -> p c t i", i=4),
+            )
+
+        def weave_dealt(op, raw, h, n):
+            s = P // n
+            nc.vector.tensor_copy(
+                out=op[0][:].rearrange("p (j s t) -> p s t j", j=PACK, t=PACK)[:, h * s : (h + 1) * s],
+                in_=raw[:].rearrange("p t (s j) -> p s t j", j=PACK),
+            )
+
+        key_scales = held.tile([P, T], U8, name="key_scales", align_bytes=64)
+        nc.gpsimd.memset(key_scales[:].bitcast(I32), 0)
+        df = [held.tile([P, M], F32, name=f"df{k}") for k in range(E // P)]
+        for k in range(E // P):
+            nc.vector.memset(df[k][:], 0.0)
+
+        q_raw = [held.tile([P, PACK, Q // 2], F32, name=f"q_raw{h}") for h in range(2)]
+        for h in range(2):
+            nc.sync.dma_start(out=q_raw[h][:], in_=by_rows(query)[:, :, h * (Q // 2) : (h + 1) * (Q // 2)])
+        key_words = held.tile([P, 2 * T], U8, name="key_words", align_bytes=64)
+        nc.sync.dma_start(out=key_words[:].bitcast(I32), in_=keys_words[0].bitcast(I32))
+        for quad in range(4):
+            nc.scalar.dma_start(
+                out=key_scales[32 * quad : 32 * quad + 4, :].bitcast(I32),
+                in_=keys_scales[0, 4 * quad : 4 * quad + 4, :].bitcast(I32),
+            )
+        q2_raw = held.tile([P, PACK, Q], F32, name="q2_raw")
+        nc.sync.dma_start(out=q2_raw[:], in_=by_rows(query2))
+        list_a = held.tile([P, I // 16], U16, name="list_a")
+        nc.sync.dma_start(list_a[:], offs)
+        pg_raw = [held.tile([P, PACK, BANK], F32, name=f"pg_raw{h}") for h in range(2)]
+        for h in range(2):
+            nc.sync.dma_start(out=pg_raw[h][:], in_=by_rows(pages)[:, :, h * BANK : (h + 1) * BANK])
+        list_h = held.tile([P, I // 16], U16, name="list_h")
+        nc.sync.dma_start(list_h[:], offs2)
+        row_factor = held.tile([P, PACK], F32, name="row_factor")
+        nc.sync.dma_start(out=row_factor[:], in_=qs.rearrange("(p t) o -> p (t o)", t=PACK))
+        fade_rows = held.tile([P, M], F32, name="fade_rows")
+        nc.sync.dma_start(out=fade_rows[:], in_=fade[0].partition_broadcast(P))
+        res = [held.tile([P, M], F32, name=f"res{k}") for k in range(E // P)]
+        for k in range(2):
+            nc.sync.dma_start(out=res[k][:], in_=old[k * P : (k + 1) * P, :])
+        msg_raw = held.tile([P, PACK, E], F32, name="msg_raw")
+        nc.sync.dma_start(out=msg_raw[:], in_=by_rows(msgs))
+        for k in range(2, 4):
+            nc.sync.dma_start(out=res[k][:], in_=old[k * P : (k + 1) * P, :])
+        list_out = held.tile([P, I // 16], U16, name="list_out")
+        nc.sync.dma_start(list_out[:], offs3)
+
+        q_op = operand("q", Q)
+        for h in range(2):
+            weave_dealt(q_op, q_raw[h], h, 2)
+        for j in range(PACK):
+            quantise(q_op, j * P, (j + 1) * P)
+
+        a_win = [held.tile([P, T], F32, name=f"a_win{j}") for j in range(PACK)]
+        sig_a = [held.tile([P, PACK, HALF], F32, name=f"sig_a{u}") for u in range(2)]
+        sig_h = [held.tile([P, PACK, HALF], F32, name=f"sig_h{u}") for u in range(2)]
+        for j in range(PACK):
+            for h in range(2):
+                bank = psum.tile([P, BANK], F32, name="bank")
+                nc.tensor.matmul_mx(
+                    out=bank[:],
+                    lhsT=q_op[1][:, j * P : (j + 1) * P].bitcast(FP8X4),
+                    lhsT_scale=q_op[2][:, j * P : (j + 1) * P],
+                    rhs=key_words[:, 2 * h * BANK : 2 * (h + 1) * BANK].bitcast(FP4X4),
+                    rhs_scale=key_scales[:, h * BANK : (h + 1) * BANK],
+                    start=True,
+                    stop=True,
+                )
+                nc.scalar.copy(out=a_win[j][:, h * BANK : (h + 1) * BANK], in_=bank[:])
+
+        q2_op = operand("q2", Q)
+        weave_dealt(q2_op, q2_raw, 0, 1)
+        quantise(q2_op, 0, Q)
+        pg_op = [operand(f"pg{h}", BANK) for h in range(2)]
+        for h in range(2):
+            weave(pg_op[h], pg_raw[h])
+            quantise(pg_op[h], 0, BANK)
+
+        for u in range(2):
+            for j in range(PACK):
+                nc.scalar.activation(
+                    sig_a[u][:, j, :], a_win[j][:].indirect(list_a[:, u * LIST_COLS : (u + 1) * LIST_COLS]), ACT.Sigmoid
+                )
+
+        h_win = [held.tile([P, Z], F32, name=f"h_win{j}") for j in range(PACK)]
+        for j in range(PACK):
+            for h in range(2):
+                bank = psum.tile([P, BANK], F32, name="bank")
+                nc.tensor.matmul_mx(
+                    out=bank[:],
+                    lhsT=q2_op[1][:, j * P : (j + 1) * P].bitcast(FP8X4),
+                    lhsT_scale=q2_op[2][:, j * P : (j + 1) * P],
+                    rhs=pg_op[h][1][:].bitcast(FP8X4),
+                    rhs_scale=pg_op[h][2][:],
+                    start=True,
+                    stop=True,
+                )
+                nc.vector.tensor_copy(out=h_win[j][:, h * BANK : (h + 1) * BANK], in_=bank[:])
+
+        for k in range(E // P):
+            nc.gpsimd.tensor_tensor(res[k][:], res[k][:], fade_rows[:], ALU.mult)
+
+        for u in range(2):
+            for j in range(PACK):
+                nc.scalar.activation(
+                    sig_h[u][:, j, :], h_win[j][:].indirect(list_h[:, u * LIST_COLS : (u + 1) * LIST_COLS]), ACT.Sigmoid
+                )
+
+        msg_op = operand("msg", E)
+        weave(msg_op, msg_raw)
+        quantise(msg_op, 0, E)
+
+        factor = row_factor[:].rearrange("p (c t i) -> p c t i", c=1, i=1).to_broadcast([P, HALF // 4, PACK, 4])
+        dl = [held.tile([P, E // P, HALF], F32, name=f"dl{u}") for u in range(2)]
+        for u in range(2):
+            w = held.tile([P, PACK, HALF], F32, name=f"w{u}")
+            for g in range(2):
+                nc.vector.tensor_tensor(
+                    w[:, 2 * g : 2 * g + 2, :], sig_a[u][:, 2 * g : 2 * g + 2, :], sig_h[u][:, 2 * g : 2 * g + 2, :], ALU.max
+                )
+            w_op = operand(f"w{u}", HALF)
+            nc.vector.tensor_tensor(
+                w_op[0][:].rearrange("p (c i t) -> p c t i", i=4, t=PACK),
+                w[:].rearrange("p t (c i) -> p c t i", i=4),
+                factor,
+                ALU.mult,
+            )
+            quantise(w_op, 0, HALF)
+            for g in range(2):
+                bank = psum.tile([P, BANK], F32, name="bank")
+                for kk in range(2):
+                    k = 2 * g + kk
+                    nc.tensor.matmul_mx(
+                        out=bank[:, kk * HALF : (kk + 1) * HALF],
+                        lhsT=msg_op[1][:, k * P : (k + 1) * P].bitcast(FP8X4),
+                        lhsT_scale=msg_op[2][:, k * P : (k + 1) * P],
+                        rhs=w_op[1][:].bitcast(FP8X4),
+                        rhs_scale=w_op[2][:],
+                        start=True,
+                        stop=True,
+                    )
+                target = dl[u][:, 2 * g : 2 * g + 2, :].rearrange("p k i -> p (k i)")
+                if u == 0:
+                    nc.scalar.copy(out=target, in_=bank[:])
+                else:
+                    nc.vector.tensor_copy(out=target, in_=bank[:])
+            for k in range(E // P):
+                places = df[k][:].indirect(list_out[:, u * LIST_COLS : (u + 1) * LIST_COLS])
+                if u == 0:
+                    nc.scalar.activation(places, dl[u][:, k, :], ACT.Copy)
+                else:
+                    nc.vector.tensor_copy(places, dl[u][:, k, :])
+                    nc.vector.tensor_tensor(res[k][:], res[k][:], df[k][:], ALU.add)
+                    nc.sync.dma_start(out=out[k * P : (k + 1) * P, :], in_=res[k][:])

@@ -1,6 +1,7 @@
 from contextlib import ExitStack
 
 import concourse.mybir as mybir
+from concourse.masks import make_identity
 
 D, T, I, Q, E, Z, M = 512, 1024, 512, 512, 512, 1024, 1024
 FLOPS = 2 * D * Q * T + 2 * D * Q * Z + 2 * Q * E * I
@@ -21,6 +22,7 @@ PACK = 4
 BANK = 512
 HALF = I // 2
 LIST_COLS = HALF // 16
+TILES = E // P
 
 
 def tile_attend_crosslarger_delivered_lean_kernel(
@@ -59,22 +61,22 @@ def tile_attend_crosslarger_delivered_lean_kernel(
                 in_=raw[:].rearrange("p t (s j) -> p s t j", j=PACK),
             )
 
-        key_scales = held.tile([P, T], U8, name="key_scales", align_bytes=64)
-        nc.gpsimd.memset(key_scales[:].bitcast(I32), 0)
-        df = [held.tile([P, M], F32, name=f"df{k}") for k in range(E // P)]
-        for k in range(E // P):
-            nc.vector.memset(df[k][:], 0.0)
+        def slots(lists, u):
+            return lists[:, u * LIST_COLS : (u + 1) * LIST_COLS]
 
         q_raw = [held.tile([P, PACK, Q // 2], F32, name=f"q_raw{h}") for h in range(2)]
-        for h in range(2):
-            nc.sync.dma_start(out=q_raw[h][:], in_=by_rows(query)[:, :, h * (Q // 2) : (h + 1) * (Q // 2)])
-        key_words = held.tile([P, 2 * T], U8, name="key_words", align_bytes=64)
-        nc.sync.dma_start(out=key_words[:].bitcast(I32), in_=keys_words[0].bitcast(I32))
+        nc.sync.dma_start(out=q_raw[0][:], in_=by_rows(query)[:, :, : Q // 2])
+        fade_cols = held.tile([P, M // P], F32, name="fade_cols")
+        nc.sync.dma_start(out=fade_cols[:], in_=fade.rearrange("o (p c) -> p (o c)", p=P))
+        nc.sync.dma_start(out=q_raw[1][:], in_=by_rows(query)[:, :, Q // 2 :])
+        scale_rows = held.tile([P, T], U8, name="scale_rows")
         for quad in range(4):
-            nc.scalar.dma_start(
-                out=key_scales[32 * quad : 32 * quad + 4, :].bitcast(I32),
+            nc.sync.dma_start(
+                out=scale_rows[32 * quad : 32 * quad + 4, :].bitcast(I32),
                 in_=keys_scales[0, 4 * quad : 4 * quad + 4, :].bitcast(I32),
             )
+        key_words = held.tile([P, 2 * T], U8, name="key_words", align_bytes=64)
+        nc.sync.dma_start(out=key_words[:].bitcast(I32), in_=keys_words[0].bitcast(I32))
         q2_raw = held.tile([P, PACK, Q], F32, name="q2_raw")
         nc.sync.dma_start(out=q2_raw[:], in_=by_rows(query2))
         list_a = held.tile([P, I // 16], U16, name="list_a")
@@ -86,27 +88,44 @@ def tile_attend_crosslarger_delivered_lean_kernel(
         nc.sync.dma_start(list_h[:], offs2)
         row_factor = held.tile([P, PACK], F32, name="row_factor")
         nc.sync.dma_start(out=row_factor[:], in_=qs.rearrange("(p t) o -> p (t o)", t=PACK))
-        fade_rows = held.tile([P, M], F32, name="fade_rows")
-        nc.sync.dma_start(out=fade_rows[:], in_=fade[0].partition_broadcast(P))
-        res = [held.tile([P, M], F32, name=f"res{k}") for k in range(E // P)]
-        for k in range(2):
-            nc.sync.dma_start(out=res[k][:], in_=old[k * P : (k + 1) * P, :])
         msg_raw = held.tile([P, PACK, E], F32, name="msg_raw")
         nc.sync.dma_start(out=msg_raw[:], in_=by_rows(msgs))
-        for k in range(2, 4):
+        res = [held.tile([P, M], F32, name=f"res{k}") for k in range(TILES)]
+        for k in range(TILES):
             nc.sync.dma_start(out=res[k][:], in_=old[k * P : (k + 1) * P, :])
         list_out = held.tile([P, I // 16], U16, name="list_out")
         nc.sync.dma_start(list_out[:], offs3)
 
+        key_scales = held.tile([P, T], U8, name="key_scales", align_bytes=64)
+        nc.vector.memset(key_scales[:].bitcast(I32), 0)
+        df = [held.tile([P, M], F32, name=f"df{k}") for k in range(TILES)]
+        for k in range(TILES):
+            nc.vector.memset(df[k][:], 0.0)
+        for quad in range(4):
+            rows = slice(32 * quad, 32 * quad + 4)
+            nc.vector.tensor_copy(out=key_scales[rows, :].bitcast(I32), in_=scale_rows[rows, :].bitcast(I32))
+
+        identity = held.tile([P, P], F32, name="identity")
+        make_identity(nc, identity[:])
+        fade_rows = held.tile([P, M], F32, name="fade_rows")
+        for g in range(2):
+            bank = psum.tile([P, PACK, P], F32, name="bank")
+            for c in range(PACK):
+                col = PACK * g + c
+                nc.tensor.transpose(bank[:, c, :], fade_cols[:, col : col + 1].to_broadcast([P, P]), identity[:])
+            nc.scalar.copy(
+                out=fade_rows[:].rearrange("p (n g c) -> p g n c", g=2, c=PACK)[:, g],
+                in_=bank[:].rearrange("p c n -> p n c"),
+            )
+
         q_op = operand("q", Q)
         for h in range(2):
             weave_dealt(q_op, q_raw[h], h, 2)
-        for j in range(PACK):
-            quantise(q_op, j * P, (j + 1) * P)
+        quantise(q_op, 0, P)
+        quantise(q_op, P, 2 * P)
+        quantise(q_op, 2 * P, Q)
 
         a_win = [held.tile([P, T], F32, name=f"a_win{j}") for j in range(PACK)]
-        sig_a = [held.tile([P, PACK, HALF], F32, name=f"sig_a{u}") for u in range(2)]
-        sig_h = [held.tile([P, PACK, HALF], F32, name=f"sig_h{u}") for u in range(2)]
         for j in range(PACK):
             for h in range(2):
                 bank = psum.tile([P, BANK], F32, name="bank")
@@ -124,53 +143,48 @@ def tile_attend_crosslarger_delivered_lean_kernel(
         q2_op = operand("q2", Q)
         weave_dealt(q2_op, q2_raw, 0, 1)
         quantise(q2_op, 0, Q)
-        pg_op = [operand(f"pg{h}", BANK) for h in range(2)]
-        for h in range(2):
-            weave(pg_op[h], pg_raw[h])
-            quantise(pg_op[h], 0, BANK)
-
-        for u in range(2):
-            for j in range(PACK):
-                nc.scalar.activation(
-                    sig_a[u][:, j, :], a_win[j][:].indirect(list_a[:, u * LIST_COLS : (u + 1) * LIST_COLS]), ACT.Sigmoid
-                )
-
         h_win = [held.tile([P, Z], F32, name=f"h_win{j}") for j in range(PACK)]
-        for j in range(PACK):
-            for h in range(2):
+        for h in range(2):
+            pg_op = operand(f"pg{h}", BANK)
+            weave(pg_op, pg_raw[h])
+            quantise(pg_op, 0, BANK)
+            for j in range(PACK):
                 bank = psum.tile([P, BANK], F32, name="bank")
                 nc.tensor.matmul_mx(
                     out=bank[:],
                     lhsT=q2_op[1][:, j * P : (j + 1) * P].bitcast(FP8X4),
                     lhsT_scale=q2_op[2][:, j * P : (j + 1) * P],
-                    rhs=pg_op[h][1][:].bitcast(FP8X4),
-                    rhs_scale=pg_op[h][2][:],
+                    rhs=pg_op[1][:].bitcast(FP8X4),
+                    rhs_scale=pg_op[2][:],
                     start=True,
                     stop=True,
                 )
-                nc.vector.tensor_copy(out=h_win[j][:, h * BANK : (h + 1) * BANK], in_=bank[:])
-
-        for k in range(E // P):
-            nc.gpsimd.tensor_tensor(res[k][:], res[k][:], fade_rows[:], ALU.mult)
-
-        for u in range(2):
-            for j in range(PACK):
-                nc.scalar.activation(
-                    sig_h[u][:, j, :], h_win[j][:].indirect(list_h[:, u * LIST_COLS : (u + 1) * LIST_COLS]), ACT.Sigmoid
-                )
+                if h == 0:
+                    nc.scalar.copy(out=h_win[j][:, h * BANK : (h + 1) * BANK], in_=bank[:])
+                else:
+                    nc.vector.tensor_copy(out=h_win[j][:, h * BANK : (h + 1) * BANK], in_=bank[:])
 
         msg_op = operand("msg", E)
         weave(msg_op, msg_raw)
         quantise(msg_op, 0, E)
 
+        def fade_old(k):
+            nc.vector.tensor_tensor(res[k][:], res[k][:], fade_rows[:], ALU.mult)
+
         factor = row_factor[:].rearrange("p (c t i) -> p c t i", c=1, i=1).to_broadcast([P, HALF // 4, PACK, 4])
-        dl = [held.tile([P, E // P, HALF], F32, name=f"dl{u}") for u in range(2)]
+        dl = [held.tile([P, TILES, HALF], F32, name=f"dl{u}") for u in range(2)]
+        w_ops = []
         for u in range(2):
+            fade_old(u)
+            sig_a = [held.tile([P, 2, HALF], F32, name=f"sig_a{u}{g}", tag=f"sig{u}{g}") for g in range(2)]
+            for j in range(PACK):
+                nc.scalar.activation(sig_a[j // 2][:, j % 2, :], a_win[j][:].indirect(slots(list_a, u)), ACT.Sigmoid)
+            sig_h = [held.tile([P, 2, HALF], F32, name=f"sig_h{u}{g}", tag=f"sig{u + 1}{g}") for g in range(2)]
+            for j in range(PACK):
+                nc.scalar.activation(sig_h[j // 2][:, j % 2, :], h_win[j][:].indirect(slots(list_h, u)), ACT.Sigmoid)
             w = held.tile([P, PACK, HALF], F32, name=f"w{u}")
             for g in range(2):
-                nc.vector.tensor_tensor(
-                    w[:, 2 * g : 2 * g + 2, :], sig_a[u][:, 2 * g : 2 * g + 2, :], sig_h[u][:, 2 * g : 2 * g + 2, :], ALU.max
-                )
+                nc.vector.tensor_tensor(w[:, 2 * g : 2 * g + 2, :], sig_a[g][:], sig_h[g][:], ALU.max)
             w_op = operand(f"w{u}", HALF)
             nc.vector.tensor_tensor(
                 w_op[0][:].rearrange("p (c i t) -> p c t i", i=4, t=PACK),
@@ -179,6 +193,11 @@ def tile_attend_crosslarger_delivered_lean_kernel(
                 ALU.mult,
             )
             quantise(w_op, 0, HALF)
+            w_ops.append(w_op)
+        fade_old(2)
+        fade_old(3)
+
+        for u in range(2):
             for g in range(2):
                 bank = psum.tile([P, BANK], F32, name="bank")
                 for kk in range(2):
@@ -187,8 +206,8 @@ def tile_attend_crosslarger_delivered_lean_kernel(
                         out=bank[:, kk * HALF : (kk + 1) * HALF],
                         lhsT=msg_op[1][:, k * P : (k + 1) * P].bitcast(FP8X4),
                         lhsT_scale=msg_op[2][:, k * P : (k + 1) * P],
-                        rhs=w_op[1][:].bitcast(FP8X4),
-                        rhs_scale=w_op[2][:],
+                        rhs=w_ops[u][1][:].bitcast(FP8X4),
+                        rhs_scale=w_ops[u][2][:],
                         start=True,
                         stop=True,
                     )
@@ -197,11 +216,15 @@ def tile_attend_crosslarger_delivered_lean_kernel(
                     nc.scalar.copy(out=target, in_=bank[:])
                 else:
                     nc.vector.tensor_copy(out=target, in_=bank[:])
-            for k in range(E // P):
-                places = df[k][:].indirect(list_out[:, u * LIST_COLS : (u + 1) * LIST_COLS])
-                if u == 0:
+            for k in range(TILES):
+                places = df[k][:].indirect(slots(list_out, u))
+                if u == 0 or k >= 2:
                     nc.scalar.activation(places, dl[u][:, k, :], ACT.Copy)
                 else:
                     nc.vector.tensor_copy(places, dl[u][:, k, :])
-                    nc.vector.tensor_tensor(res[k][:], res[k][:], df[k][:], ALU.add)
-                    nc.sync.dma_start(out=out[k * P : (k + 1) * P, :], in_=res[k][:])
+        for k in range(TILES):
+            pieces = 2 if k == TILES - 1 else 1
+            for h in range(pieces):
+                cols = slice(h * M // pieces, (h + 1) * M // pieces)
+                nc.vector.tensor_tensor(res[k][:, cols], res[k][:, cols], df[k][:, cols], ALU.add)
+                nc.sync.dma_start(out=out[k * P : (k + 1) * P, cols], in_=res[k][:, cols])

@@ -37,8 +37,8 @@ def tile_attend_crosslarger_delivered_lean_kernel(
             return x.rearrange("(p t) c -> p t c", t=PACK)
 
         def operand(name, cols):
-            grouped = held.tile([P, cols * PACK], BF16, name=name + "_bf", align_bytes=64)
-            codes = held.tile([P, cols], U32, name=name + "_codes", align_bytes=64)
+            grouped = held.tile([P, cols * PACK], BF16, name=name + "_bf", tag=name + "_bf", align_bytes=64)
+            codes = held.tile([P, cols], U32, name=name + "_codes", tag=name + "_codes", align_bytes=64)
             scales = held.tile([P, cols], U8, name=name + "_scales", align_bytes=64)
             return grouped, codes, scales
 
@@ -48,17 +48,17 @@ def tile_attend_crosslarger_delivered_lean_kernel(
                 out=codes[:, c0:c1].bitcast(FP8X4), scales=scales[:, c0:c1], in_=grouped[:, PACK * c0 : PACK * c1]
             )
 
-        def weave(op, raw):
-            nc.vector.tensor_copy(
-                out=op[0][:].rearrange("p (c i t) -> p c t i", i=4, t=PACK),
-                in_=raw[:].rearrange("p t (c i) -> p c t i", i=4),
+        def weave(copy, op, raw, c0, c1):
+            copy(
+                out=op[0][:, PACK * c0 : PACK * c1].rearrange("p (c i t) -> p c t i", i=4, t=PACK),
+                in_=raw[:, :, c0:c1].rearrange("p t (c i) -> p c t i", i=4),
             )
 
-        def weave_dealt(op, raw, h, n):
-            s = P // n
-            nc.vector.tensor_copy(
-                out=op[0][:].rearrange("p (j s t) -> p s t j", j=PACK, t=PACK)[:, h * s : (h + 1) * s],
-                in_=raw[:].rearrange("p t (s j) -> p s t j", j=PACK),
+        def weave_dealt(copy, op, raw, s0, g):
+            s1 = s0 + raw.shape[2] // PACK
+            copy(
+                out=op[0][:].rearrange("p (j s t) -> p s t j", j=PACK, t=PACK)[:, s0:s1, :, 2 * g : 2 * g + 2],
+                in_=raw[:].rearrange("p t (s j) -> p s t j", j=PACK)[:, :, :, 2 * g : 2 * g + 2],
             )
 
         def slots(lists, u):
@@ -88,11 +88,12 @@ def tile_attend_crosslarger_delivered_lean_kernel(
         nc.sync.dma_start(list_h[:], offs2)
         row_factor = held.tile([P, PACK], F32, name="row_factor")
         nc.sync.dma_start(out=row_factor[:], in_=qs.rearrange("(p t) o -> p (t o)", t=PACK))
+        old_sb = [held.tile([P, M], F32, name=f"old{k}") for k in range(TILES)]
+        nc.sync.dma_start(out=old_sb[0][:], in_=old[:P, :])
         msg_raw = held.tile([P, PACK, E], F32, name="msg_raw")
         nc.sync.dma_start(out=msg_raw[:], in_=by_rows(msgs))
-        res = [held.tile([P, M], F32, name=f"res{k}") for k in range(TILES)]
-        for k in range(TILES):
-            nc.sync.dma_start(out=res[k][:], in_=old[k * P : (k + 1) * P, :])
+        for k in range(1, TILES):
+            nc.sync.dma_start(out=old_sb[k][:], in_=old[k * P : (k + 1) * P, :])
         list_out = held.tile([P, I // 16], U16, name="list_out")
         nc.sync.dma_start(list_out[:], offs3)
 
@@ -107,6 +108,8 @@ def tile_attend_crosslarger_delivered_lean_kernel(
 
         identity = held.tile([P, P], F32, name="identity")
         make_identity(nc, identity[:])
+        unread = held.tile([P, 1], F32, name="unread")
+        nc.scalar.activation(unread[:], identity[:, 0:1], ACT.Sigmoid)
         fade_rows = held.tile([P, M], F32, name="fade_rows")
         for g in range(2):
             bank = psum.tile([P, PACK, P], F32, name="bank")
@@ -120,7 +123,8 @@ def tile_attend_crosslarger_delivered_lean_kernel(
 
         q_op = operand("q", Q)
         for h in range(2):
-            weave_dealt(q_op, q_raw[h], h, 2)
+            weave_dealt(nc.vector.tensor_copy, q_op, q_raw[h], h * (P // 2), 0)
+            weave_dealt(nc.scalar.copy, q_op, q_raw[h], h * (P // 2), 1)
         quantise(q_op, 0, P)
         quantise(q_op, P, 2 * P)
         quantise(q_op, 2 * P, Q)
@@ -141,48 +145,61 @@ def tile_attend_crosslarger_delivered_lean_kernel(
                 nc.scalar.copy(out=a_win[j][:, h * BANK : (h + 1) * BANK], in_=bank[:])
 
         q2_op = operand("q2", Q)
-        weave_dealt(q2_op, q2_raw, 0, 1)
-        quantise(q2_op, 0, Q)
-        h_win = [held.tile([P, Z], F32, name=f"h_win{j}") for j in range(PACK)]
+        for g in range(2):
+            weave_dealt(nc.vector.tensor_copy, q2_op, q2_raw, 0, g)
+        for g in range(2):
+            quantise(q2_op, g * HALF, (g + 1) * HALF)
+        pg_op = [operand(f"pg{h}", BANK) for h in range(2)]
         for h in range(2):
-            pg_op = operand(f"pg{h}", BANK)
-            weave(pg_op, pg_raw[h])
-            quantise(pg_op, 0, BANK)
+            for g in range(2):
+                weave(nc.vector.tensor_copy, pg_op[h], pg_raw[h], g * HALF, (g + 1) * HALF)
+            for g in range(2):
+                quantise(pg_op[h], g * HALF, (g + 1) * HALF)
+        h_win = [held.tile([P, Z], F32, name=f"h_win{j}") for j in range(PACK)]
+        h_banks = {}
+        for h in range(2):
             for j in range(PACK):
-                bank = psum.tile([P, BANK], F32, name="bank")
+                h_banks[j, h] = psum.tile([P, BANK], F32, name="bank")
                 nc.tensor.matmul_mx(
-                    out=bank[:],
+                    out=h_banks[j, h][:],
                     lhsT=q2_op[1][:, j * P : (j + 1) * P].bitcast(FP8X4),
                     lhsT_scale=q2_op[2][:, j * P : (j + 1) * P],
-                    rhs=pg_op[1][:].bitcast(FP8X4),
-                    rhs_scale=pg_op[2][:],
+                    rhs=pg_op[h][1][:].bitcast(FP8X4),
+                    rhs_scale=pg_op[h][2][:],
                     start=True,
                     stop=True,
                 )
-                if h == 0:
-                    nc.scalar.copy(out=h_win[j][:, h * BANK : (h + 1) * BANK], in_=bank[:])
-                else:
-                    nc.vector.tensor_copy(out=h_win[j][:, h * BANK : (h + 1) * BANK], in_=bank[:])
-
+        for j in range(PACK):
+            for h in range(2):
+                nc.vector.tensor_copy(out=h_win[j][:, h * BANK : (h + 1) * BANK], in_=h_banks[j, h][:])
         msg_op = operand("msg", E)
-        weave(msg_op, msg_raw)
-        quantise(msg_op, 0, E)
+        weave(nc.scalar.copy, msg_op, msg_raw, 0, E // 2)
+        weave(nc.vector.tensor_copy, msg_op, msg_raw, E // 2, E)
+        quantise(msg_op, 0, E // 2)
+        quantise(msg_op, E // 2, E)
 
-        def fade_old(k):
-            nc.vector.tensor_tensor(res[k][:], res[k][:], fade_rows[:], ALU.mult)
+        res = {}
+
+        def fade_old(k, tag):
+            res[k] = held.tile([P, M], F32, name=f"res{k}", tag=tag, align_bytes=64)
+            for h in range(2):
+                cols = slice(h * BANK, (h + 1) * BANK)
+                nc.gpsimd.tensor_tensor(res[k][:, cols], old_sb[k][:, cols], fade_rows[:, cols], ALU.mult)
+
+        fade_old(0, "pg1_bf")
+        fade_old(1, "pg1_codes")
 
         factor = row_factor[:].rearrange("p (c t i) -> p c t i", c=1, i=1).to_broadcast([P, HALF // 4, PACK, 4])
         dl = [held.tile([P, TILES, HALF], F32, name=f"dl{u}") for u in range(2)]
         w_ops = []
         for u in range(2):
-            fade_old(u)
             sig_a = [held.tile([P, 2, HALF], F32, name=f"sig_a{u}{g}", tag=f"sig{u}{g}") for g in range(2)]
             for j in range(PACK):
                 nc.scalar.activation(sig_a[j // 2][:, j % 2, :], a_win[j][:].indirect(slots(list_a, u)), ACT.Sigmoid)
-            sig_h = [held.tile([P, 2, HALF], F32, name=f"sig_h{u}{g}", tag=f"sig{u + 1}{g}") for g in range(2)]
+            sig_h = [held.tile([P, 2, HALF], F32, name=f"sig_h{u}{g}", tag=f"sig{2 - 2 * u}{g}") for g in range(2)]
             for j in range(PACK):
                 nc.scalar.activation(sig_h[j // 2][:, j % 2, :], h_win[j][:].indirect(slots(list_h, u)), ACT.Sigmoid)
-            w = held.tile([P, PACK, HALF], F32, name=f"w{u}")
+            w = held.tile([P, PACK, HALF], F32, name=f"w{u}", tag="w")
             for g in range(2):
                 nc.vector.tensor_tensor(w[:, 2 * g : 2 * g + 2, :], sig_a[g][:], sig_h[g][:], ALU.max)
             w_op = operand(f"w{u}", HALF)
@@ -194,8 +211,7 @@ def tile_attend_crosslarger_delivered_lean_kernel(
             )
             quantise(w_op, 0, HALF)
             w_ops.append(w_op)
-        fade_old(2)
-        fade_old(3)
+        fade_old(2, "w1_bf")
 
         for u in range(2):
             for g in range(2):
@@ -222,6 +238,7 @@ def tile_attend_crosslarger_delivered_lean_kernel(
                     nc.scalar.activation(places, dl[u][:, k, :], ACT.Copy)
                 else:
                     nc.vector.tensor_copy(places, dl[u][:, k, :])
+        fade_old(3, "w1_codes")
         for k in range(TILES):
             pieces = 2 if k == TILES - 1 else 1
             for h in range(pieces):

from contextlib import ExitStack

import concourse.mybir as mybir
from concourse.masks import make_identity

D, T, I, Q, E, Z, M = 512, 1024, 512, 512, 512, 1024, 1024
FLOPS = 2 * D * Q * T + 2 * D * Q * Z + 2 * Q * E * I

F32 = mybir.dt.float32
BF16 = mybir.dt.bfloat16
I32 = mybir.dt.int32
U32 = mybir.dt.uint32
U16 = mybir.dt.uint16
U8 = mybir.dt.uint8
FP8X4 = mybir.dt.float8_e4m3fn_x4
FP4X4 = mybir.dt.float4_e2m1fn_x4
ALU = mybir.AluOpType
ACT = mybir.ActivationFunctionType

P = 128
PACK = 4
BANK = 512
HALF = I // 2
LIST_COLS = HALF // 16
TILES = E // P


def tile_attend_crosslarger_delivered_lean_kernel(
    tc, query, query2, keys_words, keys_scales, pages, qs, msgs, old, fade, offs, offs2, offs3, out
):
    nc = tc.nc
    with ExitStack() as ctx:
        held = ctx.enter_context(tc.tile_pool(name="held", bufs=1))
        psum = ctx.enter_context(tc.psum_pool(name="psum", bufs=8))

        def by_rows(x):
            return x.rearrange("(p t) c -> p t c", t=PACK)

        def operand(name, cols):
            grouped = held.tile([P, cols * PACK], BF16, name=name + "_bf", tag=name + "_bf", align_bytes=64)
            codes = held.tile([P, cols], U32, name=name + "_codes", tag=name + "_codes", align_bytes=64)
            scales = held.tile([P, cols], U8, name=name + "_scales", align_bytes=64)
            return grouped, codes, scales

        def quantise(op, c0, c1):
            grouped, codes, scales = op
            nc.vector.quantize_mx(
                out=codes[:, c0:c1].bitcast(FP8X4), scales=scales[:, c0:c1], in_=grouped[:, PACK * c0 : PACK * c1]
            )

        def weave(copy, op, raw, c0, c1):
            copy(
                out=op[0][:, PACK * c0 : PACK * c1].rearrange("p (c i t) -> p c t i", i=4, t=PACK),
                in_=raw[:, :, c0:c1].rearrange("p t (c i) -> p c t i", i=4),
            )

        def weave_dealt(copy, op, raw, s0, g):
            s1 = s0 + raw.shape[2] // PACK
            copy(
                out=op[0][:].rearrange("p (j s t) -> p s t j", j=PACK, t=PACK)[:, s0:s1, :, 2 * g : 2 * g + 2],
                in_=raw[:].rearrange("p t (s j) -> p s t j", j=PACK)[:, :, :, 2 * g : 2 * g + 2],
            )

        def slots(lists, u):
            return lists[:, u * LIST_COLS : (u + 1) * LIST_COLS]

        q_raw = [held.tile([P, PACK, Q // 2], F32, name=f"q_raw{h}") for h in range(2)]
        nc.sync.dma_start(out=q_raw[0][:], in_=by_rows(query)[:, :, : Q // 2])
        fade_cols = held.tile([P, M // P], F32, name="fade_cols")
        nc.sync.dma_start(out=fade_cols[:], in_=fade.rearrange("o (p c) -> p (o c)", p=P))
        nc.sync.dma_start(out=q_raw[1][:], in_=by_rows(query)[:, :, Q // 2 :])
        scale_rows = held.tile([P, T], U8, name="scale_rows")
        for quad in range(4):
            nc.sync.dma_start(
                out=scale_rows[32 * quad : 32 * quad + 4, :].bitcast(I32),
                in_=keys_scales[0, 4 * quad : 4 * quad + 4, :].bitcast(I32),
            )
        key_words = held.tile([P, 2 * T], U8, name="key_words", align_bytes=64)
        nc.sync.dma_start(out=key_words[:].bitcast(I32), in_=keys_words[0].bitcast(I32))
        q2_raw = held.tile([P, PACK, Q], F32, name="q2_raw")
        nc.sync.dma_start(out=q2_raw[:], in_=by_rows(query2))
        list_a = held.tile([P, I // 16], U16, name="list_a")
        nc.sync.dma_start(list_a[:], offs)
        pg_raw = [held.tile([P, PACK, BANK], F32, name=f"pg_raw{h}") for h in range(2)]
        for h in range(2):
            nc.sync.dma_start(out=pg_raw[h][:], in_=by_rows(pages)[:, :, h * BANK : (h + 1) * BANK])
        list_h = held.tile([P, I // 16], U16, name="list_h")
        nc.sync.dma_start(list_h[:], offs2)
        row_factor = held.tile([P, PACK], F32, name="row_factor")
        nc.sync.dma_start(out=row_factor[:], in_=qs.rearrange("(p t) o -> p (t o)", t=PACK))
        old_sb = [held.tile([P, M], F32, name=f"old{k}") for k in range(TILES)]
        nc.sync.dma_start(out=old_sb[0][:], in_=old[:P, :])
        msg_raw = held.tile([P, PACK, E], F32, name="msg_raw")
        nc.sync.dma_start(out=msg_raw[:], in_=by_rows(msgs))
        for k in range(1, TILES):
            nc.sync.dma_start(out=old_sb[k][:], in_=old[k * P : (k + 1) * P, :])
        list_out = held.tile([P, I // 16], U16, name="list_out")
        nc.sync.dma_start(list_out[:], offs3)

        key_scales = held.tile([P, T], U8, name="key_scales", align_bytes=64)
        nc.vector.memset(key_scales[:].bitcast(I32), 0)
        df = [held.tile([P, M], F32, name=f"df{k}") for k in range(TILES)]
        for k in range(TILES):
            nc.vector.memset(df[k][:], 0.0)
        for quad in range(4):
            rows = slice(32 * quad, 32 * quad + 4)
            nc.vector.tensor_copy(out=key_scales[rows, :].bitcast(I32), in_=scale_rows[rows, :].bitcast(I32))

        identity = held.tile([P, P], F32, name="identity")
        make_identity(nc, identity[:])
        unread = held.tile([P, 1], F32, name="unread")
        nc.scalar.activation(unread[:], identity[:, 0:1], ACT.Sigmoid)
        fade_rows = held.tile([P, M], F32, name="fade_rows")
        for g in range(2):
            bank = psum.tile([P, PACK, P], F32, name="bank")
            for c in range(PACK):
                col = PACK * g + c
                nc.tensor.transpose(bank[:, c, :], fade_cols[:, col : col + 1].to_broadcast([P, P]), identity[:])
            nc.scalar.copy(
                out=fade_rows[:].rearrange("p (n g c) -> p g n c", g=2, c=PACK)[:, g],
                in_=bank[:].rearrange("p c n -> p n c"),
            )

        q_op = operand("q", Q)
        for h in range(2):
            weave_dealt(nc.vector.tensor_copy, q_op, q_raw[h], h * (P // 2), 0)
            weave_dealt(nc.scalar.copy, q_op, q_raw[h], h * (P // 2), 1)
        quantise(q_op, 0, P)
        quantise(q_op, P, 2 * P)
        quantise(q_op, 2 * P, Q)

        a_win = [held.tile([P, T], F32, name=f"a_win{j}") for j in range(PACK)]
        for j in range(PACK):
            for h in range(2):
                bank = psum.tile([P, BANK], F32, name="bank")
                nc.tensor.matmul_mx(
                    out=bank[:],
                    lhsT=q_op[1][:, j * P : (j + 1) * P].bitcast(FP8X4),
                    lhsT_scale=q_op[2][:, j * P : (j + 1) * P],
                    rhs=key_words[:, 2 * h * BANK : 2 * (h + 1) * BANK].bitcast(FP4X4),
                    rhs_scale=key_scales[:, h * BANK : (h + 1) * BANK],
                    start=True,
                    stop=True,
                )
                nc.scalar.copy(out=a_win[j][:, h * BANK : (h + 1) * BANK], in_=bank[:])

        q2_op = operand("q2", Q)
        for g in range(2):
            weave_dealt(nc.vector.tensor_copy, q2_op, q2_raw, 0, g)
        for g in range(2):
            quantise(q2_op, g * HALF, (g + 1) * HALF)
        pg_op = [operand(f"pg{h}", BANK) for h in range(2)]
        for h in range(2):
            for g in range(2):
                weave(nc.vector.tensor_copy, pg_op[h], pg_raw[h], g * HALF, (g + 1) * HALF)
            for g in range(2):
                quantise(pg_op[h], g * HALF, (g + 1) * HALF)
        h_win = [held.tile([P, Z], F32, name=f"h_win{j}") for j in range(PACK)]
        h_banks = {}
        for h in range(2):
            for j in range(PACK):
                h_banks[j, h] = psum.tile([P, BANK], F32, name="bank")
                nc.tensor.matmul_mx(
                    out=h_banks[j, h][:],
                    lhsT=q2_op[1][:, j * P : (j + 1) * P].bitcast(FP8X4),
                    lhsT_scale=q2_op[2][:, j * P : (j + 1) * P],
                    rhs=pg_op[h][1][:].bitcast(FP8X4),
                    rhs_scale=pg_op[h][2][:],
                    start=True,
                    stop=True,
                )
        for j in range(PACK):
            for h in range(2):
                nc.vector.tensor_copy(out=h_win[j][:, h * BANK : (h + 1) * BANK], in_=h_banks[j, h][:])
        msg_op = operand("msg", E)
        weave(nc.scalar.copy, msg_op, msg_raw, 0, E // 2)
        weave(nc.vector.tensor_copy, msg_op, msg_raw, E // 2, E)
        quantise(msg_op, 0, E // 2)
        quantise(msg_op, E // 2, E)

        res = {}

        def fade_old(k, tag):
            res[k] = held.tile([P, M], F32, name=f"res{k}", tag=tag, align_bytes=64)
            for h in range(2):
                cols = slice(h * BANK, (h + 1) * BANK)
                nc.gpsimd.tensor_tensor(res[k][:, cols], old_sb[k][:, cols], fade_rows[:, cols], ALU.mult)

        fade_old(0, "pg1_bf")
        fade_old(1, "pg1_codes")

        factor = row_factor[:].rearrange("p (c t i) -> p c t i", c=1, i=1).to_broadcast([P, HALF // 4, PACK, 4])
        dl = [held.tile([P, TILES, HALF], F32, name=f"dl{u}") for u in range(2)]
        w_ops = []
        for u in range(2):
            sig_a = [held.tile([P, 2, HALF], F32, name=f"sig_a{u}{g}", tag=f"sig{u}{g}") for g in range(2)]
            for j in range(PACK):
                nc.scalar.activation(sig_a[j // 2][:, j % 2, :], a_win[j][:].indirect(slots(list_a, u)), ACT.Sigmoid)
            sig_h = [held.tile([P, 2, HALF], F32, name=f"sig_h{u}{g}", tag=f"sig{2 - 2 * u}{g}") for g in range(2)]
            for j in range(PACK):
                nc.scalar.activation(sig_h[j // 2][:, j % 2, :], h_win[j][:].indirect(slots(list_h, u)), ACT.Sigmoid)
            w = held.tile([P, PACK, HALF], F32, name=f"w{u}", tag="w")
            for g in range(2):
                nc.vector.tensor_tensor(w[:, 2 * g : 2 * g + 2, :], sig_a[g][:], sig_h[g][:], ALU.max)
            w_op = operand(f"w{u}", HALF)
            nc.vector.tensor_tensor(
                w_op[0][:].rearrange("p (c i t) -> p c t i", i=4, t=PACK),
                w[:].rearrange("p t (c i) -> p c t i", i=4),
                factor,
                ALU.mult,
            )
            quantise(w_op, 0, HALF)
            w_ops.append(w_op)
        fade_old(2, "w1_bf")

        for u in range(2):
            for g in range(2):
                bank = psum.tile([P, BANK], F32, name="bank")
                for kk in range(2):
                    k = 2 * g + kk
                    nc.tensor.matmul_mx(
                        out=bank[:, kk * HALF : (kk + 1) * HALF],
                        lhsT=msg_op[1][:, k * P : (k + 1) * P].bitcast(FP8X4),
                        lhsT_scale=msg_op[2][:, k * P : (k + 1) * P],
                        rhs=w_ops[u][1][:].bitcast(FP8X4),
                        rhs_scale=w_ops[u][2][:],
                        start=True,
                        stop=True,
                    )
                target = dl[u][:, 2 * g : 2 * g + 2, :].rearrange("p k i -> p (k i)")
                if u == 0:
                    nc.scalar.copy(out=target, in_=bank[:])
                else:
                    nc.vector.tensor_copy(out=target, in_=bank[:])
            for k in range(TILES):
                places = df[k][:].indirect(slots(list_out, u))
                if u == 0 or k >= 2:
                    nc.scalar.activation(places, dl[u][:, k, :], ACT.Copy)
                else:
                    nc.vector.tensor_copy(places, dl[u][:, k, :])
        fade_old(3, "w1_codes")
        for k in range(TILES):
            pieces = 2 if k == TILES - 1 else 1
            for h in range(pieces):
                cols = slice(h * M // pieces, (h + 1) * M // pieces)
                nc.vector.tensor_tensor(res[k][:, cols], res[k][:, cols], df[k][:, cols], ALU.add)
                nc.sync.dma_start(out=out[k * P : (k + 1) * P, cols], in_=res[k][:, cols])
